import numpy as np
import ml_dtypes


def mxq(x, axis, fmt="e4m3"):
    dtype, down = {"e4m3": (ml_dtypes.float8_e4m3fn, 7), "e5m2": (ml_dtypes.float8_e5m2, 14)}[fmt]
    v = np.moveaxis(np.asarray(x, np.float32).astype(ml_dtypes.bfloat16).astype(np.float64), axis, -1)
    blocks = v.reshape(v.shape[:-1] + (-1, 32))
    amax = np.abs(blocks).max(-1, keepdims=True)
    byte = np.maximum(np.where(amax > 0, np.frexp(amax)[1] - 1 + 127, 0) - down, 1)
    scale = np.exp2(byte - 127.0)
    codes = (blocks / scale).astype(np.float32).astype(dtype).astype(np.float64)
    return np.moveaxis((codes * scale).reshape(v.shape), -1, axis)


WIDE = False


def mx_kscale(k):
    if not WIDE:
        return np.ones(k)
    levels = np.array([10, -10, 5, -5, 0])
    if k % 512:
        return np.exp2(np.random.permutation(np.resize(levels, k // 32))).repeat(32)
    a = np.empty((k // 512, 16))
    for p in range(k // 512):
        a[p, :8] = np.random.permutation(np.resize(levels, 8))
        for g in range(8):
            far = levels[np.abs(levels - a[p, g]) >= 10]
            a[p, g + 8] = far[np.random.randint(len(far))]
    return np.exp2(a.ravel()).repeat(32)


def f64(x):
    return np.asarray(x).astype(np.float64)


def striped(idx):
    return np.tile(np.asarray(idx).reshape(-1, 16).T, (8, 1)).astype(np.uint16)


def unstriped(offs):
    return offs[:16].T.reshape(-1).astype(np.int64)


E2M1 = np.array([0.0, 0.5, 1.0, 1.5, 2.0, 3.0, 4.0, 6.0, -0.0, -0.5, -1.0, -1.5, -2.0, -3.0, -4.0, -6.0])


def pack_weight(w, fmt):
    k, n = w.shape
    w = f64(np.asarray(w, np.float32).astype(ml_dtypes.bfloat16)).reshape(k // 32, 32, n)
    amax = np.abs(w).max(1)
    if fmt == "e4m3":
        byte = np.frexp(amax)[1] - 1 + 127 - 7
    else:
        mant, ex = np.frexp(amax / 6.0)
        byte = np.where(mant > 0.5, ex, ex - 1) + 127
    byte = np.clip(np.where(amax > 0, byte, 1), 1, 254)
    scaled = (w * np.exp2(127.0 - byte)[:, None, :]).reshape(k, n).astype(np.float32)
    by_word = np.ascontiguousarray(scaled.reshape(k // 512, 128, 4, n).transpose(0, 1, 3, 2))
    if fmt == "e4m3":
        words = by_word.astype(ml_dtypes.float8_e4m3fn).view(np.uint8)
    else:
        c = by_word.astype(ml_dtypes.float4_e2m1fn).view(np.uint8) & 0xF
        words = (c[..., 0::2] | (c[..., 1::2] << 4)).reshape(k // 512, 128, 2 * n)
    return np.ascontiguousarray(words), np.ascontiguousarray(byte.astype(np.uint8).reshape(k // 512, 16, n))


def unpack_weight(words, scales, fmt):
    g, _, n = scales.shape
    words = np.ascontiguousarray(words).reshape(g, 128, n, -1)
    if fmt == "e4m3":
        vals = words.view(ml_dtypes.float8_e4m3fn).astype(np.float64)
    else:
        nib = np.empty((g, 128, n, 4), np.uint8)
        nib[..., 0::2] = words & 0xF
        nib[..., 1::2] = words >> 4
        vals = E2M1[nib]
    vals = vals * np.repeat(np.exp2(scales.astype(np.float64) - 127.0), 8, axis=1)[..., None]
    return vals.transpose(0, 1, 3, 2).reshape(g * 512, n)


def bf(x):
    return np.asarray(x, np.float32).astype(ml_dtypes.bfloat16)


def planes(Y):
    r, m = Y.shape
    b = f64(bf(Y)).reshape(r // 32, 32, m)
    amax = np.abs(b).max(1)
    byte = np.clip(np.where(amax > 0, np.frexp(amax)[1] - 1 + 127 - 7, 1), 1, 254)
    codes = (b * np.exp2(127.0 - byte)[:, None, :]).reshape(r, m).astype(np.float32).astype(ml_dtypes.float8_e4m3fn).view(np.uint8)
    words = codes.reshape(r // 512, 128, 4, m).transpose(0, 1, 3, 2)
    return np.ascontiguousarray(words), np.ascontiguousarray(byte.astype(np.uint8).reshape(r // 512, 16, m))


D, E, T, I, Q = 512, 512, 2048, 512, 256


def setup_inputs():
    n = np.random.standard_normal
    idx = np.random.permutation(T)[:I]
    fd = mx_kscale(D)
    fi = mx_kscale(I)
    ti = np.ones(T)
    ti[idx] = fi
    keysp = pack_weight(n((D, T)) / fd[:, None], "e2m1")
    return {
        "query": (n((D, Q)) * 0.5 / np.sqrt(D) * fd[:, None]).astype(np.float32),
        "dquery": (n((D, Q)) * 1.0 / np.sqrt(D) * fd[:, None]).astype(np.float32),
        "keys_words": keysp[0],
        "keys_scales": keysp[1],
        "size": (np.random.uniform(4.0, 16.0, (1, I)) * fi).astype(np.float32),
        "vals": (n((E, T)) / ti).astype(np.float32),
        "offs": striped(idx),
    }


def reference(query, dquery, keys_words, keys_scales, size, vals, offs):
    idx = unstriped(offs)
    keysu = unpack_weight(keys_words, keys_scales, "e2m1")
    queryq = mxq(f64(query), 0, "e4m3")
    keysidxg = keysu[:, idx]
    a = queryq.T @ keysidxg
    dqueryq = mxq(f64(dquery), 0, "e4m3")
    b = dqueryq.T @ keysidxg
    p = np.exp(a - np.max(a, axis=1, keepdims=True))
    w = p / np.sum(p, axis=1, keepdims=True)
    dw = w * (b - np.sum(w * b, axis=1, keepdims=True)) * f64(size)
    wt = dw.T
    vt = f64(vals)[:, idx].T
    vtq = mxq(vt, 0, "e4m3")
    wtq = mxq(wt, 0, "e4m3")
    o = vtq.T @ wtq
    words, scales = planes(o)
    return o, words, scales

@@ -1,0 +1,202 @@
+from contextlib import ExitStack
+
+import concourse.mybir as mybir
+from concourse.masks import make_identity
+
+D, E, T, I, Q = 512, 512, 2048, 512, 256
+P = 128
+PACK = 4
+HALVES = Q // P
+FLOPS = 2 * (2 * D * Q * I + I * E * Q)
+
+F32 = mybir.dt.float32
+BF16 = mybir.dt.bfloat16
+I32 = mybir.dt.int32
+U32 = mybir.dt.uint32
+U16 = mybir.dt.uint16
+U8 = mybir.dt.uint8
+FP8X4 = mybir.dt.float8_e4m3fn_x4
+FP4X4 = mybir.dt.float4_e2m1fn_x4
+ALU = mybir.AluOpType
+ACT = mybir.ActivationFunctionType
+AXIS = mybir.AxisListType
+
+
+def tile_attend_readtangent_pl_kernel(tc, query, dquery, keys_words, keys_scales, size, vals, offs, out_0, out_1, out_2):
+    nc = tc.nc
+    with ExitStack() as ctx:
+        sb = ctx.enter_context(tc.tile_pool(name="sb", bufs=1))
+        ps = ctx.enter_context(tc.psum_pool(name="ps", bufs=1))
+
+        def tile(name, shape, dtype, tag=None):
+            return sb.tile(shape, dtype, name=name, tag=tag or name, align_bytes=64)
+
+        def quantise(name, grouped, columns, tag=None):
+            codes = tile(name + "_codes", [P, columns], U32, tag)
+            scales = tile(name + "_scales", [P, columns], U8)
+            nc.vector.quantize_mx(out=codes[:].bitcast(FP8X4), scales=scales[:], in_=grouped)
+            return codes, scales
+
+        offsets = sb.tile([P, I // 16], U16, name="offsets")
+        key_bytes = tile("key_bytes", [P, T], U8)
+        nc.gpsimd.memset(key_bytes[:].bitcast(I32), 0)
+        nc.sync.dma_start(offsets[:], offs)
+        slot_size = tile("slot_size", [P, PACK], F32)
+        nc.sync.dma_start(slot_size[:], size.rearrange("o (s r) -> s (o r)", r=PACK))
+        for quad in range(4):
+            nc.sync.dma_start(key_bytes[32 * quad : 32 * quad + 4, :].bitcast(I32), keys_scales[0, 4 * quad : 4 * quad + 4, :].bitcast(I32))
+        key_words = tile("key_words", [P, T], U16)
+        nc.sync.dma_start(key_words[:].bitcast(I32), keys_words[0].bitcast(I32))
+        q_raw = tile("q_raw", [P, PACK, Q], F32)
+        nc.sync.dma_start(q_raw[:], query.rearrange("(p j) q -> p j q", j=PACK))
+        dq_raw = tile("dq_raw", [P, PACK, Q], F32)
+        nc.sync.dma_start(dq_raw[:], dquery.rearrange("(p j) q -> p j q", j=PACK))
+        vals_rows = vals.rearrange("(p t) c -> t p c", t=PACK)
+        pools = []
+        for t in range(PACK):
+            pool_t = tile("vals_pool%d" % t, [P, T], F32)
+            nc.sync.dma_start(pool_t[:], vals_rows[t])
+            pools.append(pool_t)
+
+        ident = tile("ident", [P, P], F32)
+        make_identity(nc, ident[:])
+        warm = tile("warm", [P, 1], F32)
+        nc.gpsimd.memset(warm[:], 0.0)
+        warm_out = tile("warm_out", [P, 1], F32)
+        nc.scalar.activation(warm_out[:], warm[:], ACT.Exp)
+
+        kb = tile("kb", [P, I], U8)
+        nc.vector.tensor_copy(kb[:], key_bytes[:].indirect(offsets[:]))
+
+        def interleave(name, raw, on_vector):
+            grouped = tile(name + "_bf", [P, Q, PACK], BF16)
+            for copy, cols in ((nc.vector.tensor_copy, slice(0, on_vector)), (nc.scalar.copy, slice(on_vector, Q))):
+                if cols.stop > cols.start:
+                    copy(
+                        grouped[:, cols, :].rearrange("p (c i) j -> p c j i", i=4),
+                        raw[:, :, cols].rearrange("p j (c i) -> p c j i", i=4),
+                    )
+            return grouped[:].rearrange("p q j -> p (q j)")
+
+        kw = tile("kw", [P, I], U16)
+        nc.vector.tensor_copy(kw[:], key_words[:].indirect(offsets[:]))
+        q_bf = interleave("q", q_raw, 160)
+        dq_bf = interleave("dq", dq_raw, 0)
+        q_mx = quantise("q", q_bf, Q)
+
+        def scores(tag, operand, h):
+            codes, scales = operand
+            bank = ps.tile([P, I], F32, name=tag, tag=tag)
+            cols = slice(h * P, (h + 1) * P)
+            nc.tensor.matmul_mx(out=bank[:], lhsT=codes[:, cols].bitcast(FP8X4), lhsT_scale=scales[:, cols],
+                                rhs=kw[:].bitcast(FP4X4), rhs_scale=kb[:], start=True, stop=True)
+            return bank
+
+        a = [scores("a%d" % h, q_mx, h) for h in range(HALVES)]
+        neg_max = [tile("neg_max%d" % h, [P, 1], F32) for h in range(HALVES)]
+        nc.vector.tensor_reduce(neg_max[0][:], a[0][:], AXIS.X, ALU.max, negate=True)
+        dq_mx = quantise("dq", dq_bf, Q)
+        b = [scores("b%d" % h, dq_mx, h) for h in range(HALVES)]
+        nc.vector.tensor_reduce(neg_max[1][:], a[1][:], AXIS.X, ALU.max, negate=True)
+
+        p_dealt, inv_sum = [], []
+        for h in range(HALVES):
+            p_h = tile("p%d" % h, [P, PACK, P], F32)
+            row_sum = tile("row_sum%d" % h, [P, 1], F32)
+            nc.scalar.activation(p_h[:], a[h][:].rearrange("q (s r) -> q r s", r=PACK), ACT.Exp, bias=neg_max[h][:], accum_out=row_sum[:])
+            inv = tile("inv_sum%d" % h, [P, 1], F32)
+            nc.vector.reciprocal(inv[:], row_sum[:])
+            p_dealt.append(p_h)
+            inv_sum.append(inv)
+
+        picks = []
+
+        def gather_values(t):
+            picked = tile("picked%d" % t, [P, I], BF16)
+            nc.vector.tensor_copy(picked[:], pools[t][:].indirect(offsets[:]))
+            picks.append(picked)
+
+        def turn_values(t, bank):
+            turned = ps.tile([P, 2, P], F32, name="turned%d" % t, tag=bank)
+            words = picks[t][:].bitcast(F32)
+            for u in range(2):
+                nc.tensor.transpose(turned[:, u, :], words[:, u::2], ident[:])
+            grouped = tile("v_bf%d" % t, [P, P, 2], F32)
+            nc.scalar.copy(grouped[:], turned[:].rearrange("s u e -> s e u"))
+            return grouped[:].rearrange("s e u -> s (e u)").bitcast(BF16)
+
+        means = []
+
+        def tangent(h):
+            wb = tile("wb%d" % h, [P, PACK, P], F32)
+            mean = tile("mean%d" % h, [P, 1], F32)
+            nc.vector.scalar_tensor_tensor(wb[:], b[h][:].rearrange("q (s r) -> q r s", r=PACK), inv_sum[h][:], p_dealt[h][:],
+                                           ALU.mult, ALU.mult, accum_out=mean[:])
+            factor = tile("factor%d" % h, [P, 1], F32)
+            neg_inv = tile("neg_inv%d" % h, [P, 1], F32)
+            nc.scalar.activation(neg_inv[:], inv_sum[h][:], ACT.Copy, scale=-1.0)
+            nc.scalar.activation(factor[:], mean[:], ACT.Copy, scale=neg_inv[:])
+            means.append(mean)
+            wm = tile("wm%d" % h, [P, PACK, P], F32)
+            nc.scalar.activation(wm[:], p_dealt[h][:], ACT.Copy, scale=factor[:])
+            turned = ps.tile([P, PACK, P], F32, name="dw%d" % h, tag="a%d" % h)
+            for r in range(PACK):
+                nc.tensor.matmul(turned[:, r, :], wb[:, r, :], ident[:], start=(r == 0), stop=False, is_transpose=True)
+            for r in range(PACK):
+                nc.tensor.matmul(turned[:, r, :], wm[:, r, :], ident[:], start=False, stop=(r == PACK - 1), is_transpose=True)
+            return turned
+
+        def weigh(h, turned):
+            grouped = tile("w_bf%d" % h, [P, P, PACK], BF16, "vals_pool1" if h == 0 else None)
+            nc.vector.tensor_tensor(grouped[:], turned[:].rearrange("s r q -> s q r"),
+                                    slot_size[:].unsqueeze(1).to_broadcast([P, P, PACK]), ALU.mult)
+            return grouped[:].rearrange("s q r -> s (q r)")
+
+        gather_values(0)
+        dw = [tangent(h) for h in range(HALVES)]
+        gather_values(1)
+        v_bf = [turn_values(0, "b1")]
+        w_bf = [weigh(h, dw[h]) for h in range(HALVES)]
+        v_bf.append(turn_values(1, "a0"))
+        gather_values(2)
+        v_bf.append(turn_values(2, "a1"))
+        w_mx = [quantise("w%d" % h, w_bf[h], P, "vals_pool2" if h == 0 else None) for h in range(HALVES)]
+
+        o_bank = [ps.tile([P, PACK, P], F32, name="o%d" % h, tag="o%d" % h) for h in range(HALVES)]
+
+        def read_out(t):
+            v_codes, v_scales = quantise("v%d" % t, v_bf[t], P, "vals_pool3" if t == 2 else None)
+            for h in range(HALVES):
+                w_codes, w_scales = w_mx[h]
+                nc.tensor.matmul_mx(out=o_bank[h][:, t, :], lhsT=v_codes[:].bitcast(FP8X4), lhsT_scale=v_scales[:],
+                                    rhs=w_codes[:].bitcast(FP8X4), rhs_scale=w_scales[:], start=True, stop=True)
+
+        out_rows = out_0.rearrange("(p t) q -> p t q", t=PACK)
+        last = PACK - 1
+
+        def hand_out(name, first, stop):
+            rows = tile(name, [P, stop - first, Q], F32)
+            for h in range(HALVES):
+                nc.scalar.copy(rows[:, :, h * P : (h + 1) * P], o_bank[h][:, first:stop, :])
+            nc.sync.dma_start(out_rows[:, first:stop, :], rows[:])
+
+        read_out(0)
+        read_out(1)
+        hand_out("o_01", 0, 2)
+        gather_values(last)
+        v_bf.append(turn_values(last, "b0"))
+        read_out(2)
+        hand_out("o_2", 2, 3)
+        read_out(last)
+        o_bf = tile("o_bf", [P, Q, PACK], BF16)
+        nc.vector.tensor_copy(o_bf[:, 0:P, :], o_bank[0][:].rearrange("p t q -> p q t"))
+        nc.scalar.copy(o_bf[:, P:Q, :], o_bank[1][:].rearrange("p t q -> p q t"))
+        o_codes, o_scales = quantise("o", o_bf[:].rearrange("p q t -> p (q t)"), Q)
+        o_last = tile("o_last", [P, Q], F32)
+        for h in reversed(range(HALVES)):
+            nc.scalar.copy(o_last[:, h * P : (h + 1) * P], o_bank[h][:, last, :])
+        nc.scalar.dma_start(out_rows[:, last, :], o_last[:])
+        nc.sync.dma_start(out_1[0].rearrange("p c r -> p (c r)").bitcast(I32), o_codes[:].bitcast(I32))
+        for quad in range(4):
+            queue = nc.sync if quad % 2 == 0 else nc.scalar
+            queue.dma_start(out_2[0, 4 * quad : 4 * quad + 4, :].bitcast(I32), o_scales[32 * quad : 32 * quad + 4, :].bitcast(I32))

@@ -28,8 +28,12 @@ def tile_attend_readtangent_pl_kernel(tc, query, dquery, keys_words, keys_scales
         sb = ctx.enter_context(tc.tile_pool(name="sb", bufs=1))
         ps = ctx.enter_context(tc.psum_pool(name="ps", bufs=1))
 
-        def tile(name, shape, dtype, tag=None):
-            return sb.tile(shape, dtype, name=name, tag=tag or name, align_bytes=64)
+        shared = ctx.enter_context(tc.tile_pool(name="shared", bufs=1))
+
+        def tile(name, shape, dtype, place=None):
+            if place is None:
+                return sb.tile(shape, dtype, name=name, align_bytes=64)
+            return shared.tile(shape, dtype, name=name, align_bytes=64, offset=place[0] * T * 4 + place[1] * 2048)
 
         def quantise(name, grouped, columns, tag=None):
             codes = tile(name + "_codes", [P, columns], U32, tag)
@@ -47,67 +51,65 @@ def tile_attend_readtangent_pl_kernel(tc, query, dquery, keys_words, keys_scales
             nc.sync.dma_start(key_bytes[32 * quad : 32 * quad + 4, :].bitcast(I32), keys_scales[0, 4 * quad : 4 * quad + 4, :].bitcast(I32))
         key_words = tile("key_words", [P, T], U16)
         nc.sync.dma_start(key_words[:].bitcast(I32), keys_words[0].bitcast(I32))
-        q_raw = tile("q_raw", [P, PACK, Q], F32)
-        nc.sync.dma_start(q_raw[:], query.rearrange("(p j) q -> p j q", j=PACK))
+        q_raw = []
+        for h in range(HALVES):
+            q_half = tile("q_raw%d" % h, [P, PACK, P], F32)
+            nc.sync.dma_start(q_half[:], query.rearrange("(p j) q -> p j q", j=PACK)[:, :, h * P : (h + 1) * P])
+            q_raw.append(q_half)
         dq_raw = tile("dq_raw", [P, PACK, Q], F32)
         nc.sync.dma_start(dq_raw[:], dquery.rearrange("(p j) q -> p j q", j=PACK))
         vals_rows = vals.rearrange("(p t) c -> t p c", t=PACK)
         pools = []
         for t in range(PACK):
-            pool_t = tile("vals_pool%d" % t, [P, T], F32)
+            pool_t = tile("vals_pool%d" % t, [P, T], F32, (t, 0))
             nc.sync.dma_start(pool_t[:], vals_rows[t])
             pools.append(pool_t)
 
         ident = tile("ident", [P, P], F32)
         make_identity(nc, ident[:])
-        warm = tile("warm", [P, 1], F32)
-        nc.gpsimd.memset(warm[:], 0.0)
-        warm_out = tile("warm_out", [P, 1], F32)
-        nc.scalar.activation(warm_out[:], warm[:], ACT.Exp)
 
         kb = tile("kb", [P, I], U8)
         nc.vector.tensor_copy(kb[:], key_bytes[:].indirect(offsets[:]))
 
-        def interleave(name, raw, on_vector):
-            grouped = tile(name + "_bf", [P, Q, PACK], BF16)
-            for copy, cols in ((nc.vector.tensor_copy, slice(0, on_vector)), (nc.scalar.copy, slice(on_vector, Q))):
-                if cols.stop > cols.start:
-                    copy(
-                        grouped[:, cols, :].rearrange("p (c i) j -> p c j i", i=4),
-                        raw[:, :, cols].rearrange("p j (c i) -> p c j i", i=4),
-                    )
+        def interleave(name, rows):
+            grouped = tile(name, [P, P, PACK], BF16)
+            nc.scalar.activation(
+                grouped[:].rearrange("p (c i) j -> p c j i", i=4),
+                rows.rearrange("p j (c i) -> p c j i", i=4),
+                ACT.Copy,
+            )
             return grouped[:].rearrange("p q j -> p (q j)")
 
         kw = tile("kw", [P, I], U16)
         nc.vector.tensor_copy(kw[:], key_words[:].indirect(offsets[:]))
-        q_bf = interleave("q", q_raw, 160)
-        dq_bf = interleave("dq", dq_raw, 0)
-        q_mx = quantise("q", q_bf, Q)
+        q_bf = [interleave("q_bf%d" % h, q_raw[h][:]) for h in range(HALVES)]
+        dq_bf = [interleave("dq_bf%d" % h, dq_raw[:, :, h * P : (h + 1) * P]) for h in range(HALVES)]
 
-        def scores(tag, operand, h):
-            codes, scales = operand
+        def scores(tag, grouped):
+            codes, scales = quantise(tag, grouped, P)
             bank = ps.tile([P, I], F32, name=tag, tag=tag)
-            cols = slice(h * P, (h + 1) * P)
-            nc.tensor.matmul_mx(out=bank[:], lhsT=codes[:, cols].bitcast(FP8X4), lhsT_scale=scales[:, cols],
+            nc.tensor.matmul_mx(out=bank[:], lhsT=codes[:].bitcast(FP8X4), lhsT_scale=scales[:],
                                 rhs=kw[:].bitcast(FP4X4), rhs_scale=kb[:], start=True, stop=True)
             return bank
 
-        a = [scores("a%d" % h, q_mx, h) for h in range(HALVES)]
-        neg_max = [tile("neg_max%d" % h, [P, 1], F32) for h in range(HALVES)]
-        nc.vector.tensor_reduce(neg_max[0][:], a[0][:], AXIS.X, ALU.max, negate=True)
-        dq_mx = quantise("dq", dq_bf, Q)
-        b = [scores("b%d" % h, dq_mx, h) for h in range(HALVES)]
-        nc.vector.tensor_reduce(neg_max[1][:], a[1][:], AXIS.X, ALU.max, negate=True)
+        a = [scores("a%d" % h, q_bf[h]) for h in range(HALVES)]
+        p_dealt, inv_sum, b = [], [], []
 
-        p_dealt, inv_sum = [], []
-        for h in range(HALVES):
-            p_h = tile("p%d" % h, [P, PACK, P], F32)
+        def softmax(h):
+            neg_max = tile("neg_max%d" % h, [P, 1], F32)
+            nc.vector.tensor_reduce(neg_max[:], a[h][:], AXIS.X, ALU.max, negate=True)
+            p_h = tile("p%d" % h, [P, PACK, P], F32, (PACK, h))
             row_sum = tile("row_sum%d" % h, [P, 1], F32)
-            nc.scalar.activation(p_h[:], a[h][:].rearrange("q (s r) -> q r s", r=PACK), ACT.Exp, bias=neg_max[h][:], accum_out=row_sum[:])
+            nc.scalar.activation(p_h[:], a[h][:].rearrange("q (s r) -> q r s", r=PACK), ACT.Exp, bias=neg_max[:], accum_out=row_sum[:])
             inv = tile("inv_sum%d" % h, [P, 1], F32)
             nc.vector.reciprocal(inv[:], row_sum[:])
             p_dealt.append(p_h)
             inv_sum.append(inv)
+
+        softmax(0)
+        b.append(scores("b0", dq_bf[0]))
+        softmax(1)
+        b.append(scores("b1", dq_bf[1]))
 
         picks = []
 
@@ -146,30 +148,39 @@ def tile_attend_readtangent_pl_kernel(tc, query, dquery, keys_words, keys_scales
                 nc.tensor.matmul(turned[:, r, :], wm[:, r, :], ident[:], start=False, stop=(r == PACK - 1), is_transpose=True)
             return turned
 
-        def weigh(h, turned):
-            grouped = tile("w_bf%d" % h, [P, P, PACK], BF16, "vals_pool1" if h == 0 else None)
-            nc.vector.tensor_tensor(grouped[:], turned[:].rearrange("s r q -> s q r"),
-                                    slot_size[:].unsqueeze(1).to_broadcast([P, P, PACK]), ALU.mult)
-            return grouped[:].rearrange("s q r -> s (q r)")
+        w_bf = tile("w_bf", [P, Q, PACK], BF16)
 
-        gather_values(0)
+        def weigh(h, turned):
+            nc.vector.tensor_tensor(w_bf[:, h * P : (h + 1) * P, :], turned[:].rearrange("s r q -> s q r"),
+                                    slot_size[:].unsqueeze(1).to_broadcast([P, P, PACK]), ALU.mult)
+
         dw = [tangent(h) for h in range(HALVES)]
+        pool0_bf = tile("pool0_bf", [P, T], BF16)
+        nc.vector.tensor_copy(pool0_bf[:, T // 2 :], pools[0][:, T // 2 :])
+        for c in range(2):
+            nc.scalar.copy(pool0_bf[:, 512 * c : 512 * (c + 1)], pools[0][:, 512 * c : 512 * (c + 1)])
+        picked0 = tile("picked0", [P, I], BF16, (PACK, 1))
+        picks.append(picked0)
         gather_values(1)
-        v_bf = [turn_values(0, "b1")]
-        w_bf = [weigh(h, dw[h]) for h in range(HALVES)]
-        v_bf.append(turn_values(1, "a0"))
+        for h in range(HALVES):
+            weigh(h, dw[h])
+        v_bf = {1: turn_values(1, "b0")}
+        nc.scalar.activation(picked0[:], pool0_bf[:].indirect(offsets[:]), ACT.Copy)
+        v_mx = {1: quantise("v1", v_bf[1], P)}
+        w_codes, w_scales = quantise("w", w_bf[:].rearrange("s q r -> s (q r)"), Q)
+        v_bf[0] = turn_values(0, "v0")
         gather_values(2)
-        v_bf.append(turn_values(2, "a1"))
-        w_mx = [quantise("w%d" % h, w_bf[h], P, "vals_pool2" if h == 0 else None) for h in range(HALVES)]
+        v_mx[0] = quantise("v0", v_bf[0], P)
+        v_bf[2] = turn_values(2, "b1")
 
         o_bank = [ps.tile([P, PACK, P], F32, name="o%d" % h, tag="o%d" % h) for h in range(HALVES)]
 
         def read_out(t):
-            v_codes, v_scales = quantise("v%d" % t, v_bf[t], P, "vals_pool3" if t == 2 else None)
+            v_codes, v_scales = v_mx[t]
             for h in range(HALVES):
-                w_codes, w_scales = w_mx[h]
+                cols = slice(h * P, (h + 1) * P)
                 nc.tensor.matmul_mx(out=o_bank[h][:, t, :], lhsT=v_codes[:].bitcast(FP8X4), lhsT_scale=v_scales[:],
-                                    rhs=w_codes[:].bitcast(FP8X4), rhs_scale=w_scales[:], start=True, stop=True)
+                                    rhs=w_codes[:, cols].bitcast(FP8X4), rhs_scale=w_scales[:, cols], start=True, stop=True)
 
         out_rows = out_0.rearrange("(p t) q -> p t q", t=PACK)
         last = PACK - 1
@@ -180,13 +191,15 @@ def tile_attend_readtangent_pl_kernel(tc, query, dquery, keys_words, keys_scales
                 nc.scalar.copy(rows[:, :, h * P : (h + 1) * P], o_bank[h][:, first:stop, :])
             nc.sync.dma_start(out_rows[:, first:stop, :], rows[:])
 
-        read_out(0)
         read_out(1)
+        read_out(0)
         hand_out("o_01", 0, 2)
         gather_values(last)
-        v_bf.append(turn_values(last, "b0"))
+        v_bf[last] = turn_values(last, "v3")
+        v_mx[2] = quantise("v2", v_bf[2], P, (last, 0))
         read_out(2)
         hand_out("o_2", 2, 3)
+        v_mx[last] = quantise("v3", v_bf[last], P)
         read_out(last)
         o_bf = tile("o_bf", [P, Q, PACK], BF16)
         nc.vector.tensor_copy(o_bf[:, 0:P, :], o_bank[0][:].rearrange("p t q -> p q t"))

@@ -51,11 +51,8 @@ def tile_attend_readtangent_pl_kernel(tc, query, dquery, keys_words, keys_scales
             nc.sync.dma_start(key_bytes[32 * quad : 32 * quad + 4, :].bitcast(I32), keys_scales[0, 4 * quad : 4 * quad + 4, :].bitcast(I32))
         key_words = tile("key_words", [P, T], U16)
         nc.sync.dma_start(key_words[:].bitcast(I32), keys_words[0].bitcast(I32))
-        q_raw = []
-        for h in range(HALVES):
-            q_half = tile("q_raw%d" % h, [P, PACK, P], F32)
-            nc.sync.dma_start(q_half[:], query.rearrange("(p j) q -> p j q", j=PACK)[:, :, h * P : (h + 1) * P])
-            q_raw.append(q_half)
+        q_raw = tile("q_raw", [P, PACK, Q], F32)
+        nc.sync.dma_start(q_raw[:], query.rearrange("(p j) q -> p j q", j=PACK))
         dq_raw = tile("dq_raw", [P, PACK, Q], F32)
         nc.sync.dma_start(dq_raw[:], dquery.rearrange("(p j) q -> p j q", j=PACK))
         vals_rows = vals.rearrange("(p t) c -> t p c", t=PACK)
@@ -71,18 +68,19 @@ def tile_attend_readtangent_pl_kernel(tc, query, dquery, keys_words, keys_scales
         kb = tile("kb", [P, I], U8)
         nc.vector.tensor_copy(kb[:], key_bytes[:].indirect(offsets[:]))
 
-        def interleave(name, rows):
+        def interleave(name, rows, on_vector=False):
             grouped = tile(name, [P, P, PACK], BF16)
-            nc.scalar.activation(
-                grouped[:].rearrange("p (c i) j -> p c j i", i=4),
-                rows.rearrange("p j (c i) -> p c j i", i=4),
-                ACT.Copy,
-            )
+            dst = grouped[:].rearrange("p (c i) j -> p c j i", i=4)
+            src = rows.rearrange("p j (c i) -> p c j i", i=4)
+            if on_vector:
+                nc.vector.tensor_copy(dst, src)
+            else:
+                nc.scalar.activation(dst, src, ACT.Copy)
             return grouped[:].rearrange("p q j -> p (q j)")
 
         kw = tile("kw", [P, I], U16)
         nc.vector.tensor_copy(kw[:], key_words[:].indirect(offsets[:]))
-        q_bf = [interleave("q_bf%d" % h, q_raw[h][:]) for h in range(HALVES)]
+        q_bf = [interleave("q_bf%d" % h, q_raw[:, :, h * P : (h + 1) * P], h == 0) for h in range(HALVES)]
         dq_bf = [interleave("dq_bf%d" % h, dq_raw[:, :, h * P : (h + 1) * P]) for h in range(HALVES)]
 
         def scores(tag, grouped):
@@ -98,9 +96,9 @@ def tile_attend_readtangent_pl_kernel(tc, query, dquery, keys_words, keys_scales
         def softmax(h):
             neg_max = tile("neg_max%d" % h, [P, 1], F32)
             nc.vector.tensor_reduce(neg_max[:], a[h][:], AXIS.X, ALU.max, negate=True)
-            p_h = tile("p%d" % h, [P, PACK, P], F32, (PACK, h))
+            p_h = tile("p%d" % h, [P, I], F32, (PACK, h))
             row_sum = tile("row_sum%d" % h, [P, 1], F32)
-            nc.scalar.activation(p_h[:], a[h][:].rearrange("q (s r) -> q r s", r=PACK), ACT.Exp, bias=neg_max[:], accum_out=row_sum[:])
+            nc.scalar.activation(p_h[:], a[h][:], ACT.Exp, bias=neg_max[:], accum_out=row_sum[:])
             inv = tile("inv_sum%d" % h, [P, 1], F32)
             nc.vector.reciprocal(inv[:], row_sum[:])
             p_dealt.append(p_h)
@@ -132,7 +130,8 @@ def tile_attend_readtangent_pl_kernel(tc, query, dquery, keys_words, keys_scales
         def tangent(h):
             wb = tile("wb%d" % h, [P, PACK, P], F32)
             mean = tile("mean%d" % h, [P, 1], F32)
-            nc.vector.scalar_tensor_tensor(wb[:], b[h][:].rearrange("q (s r) -> q r s", r=PACK), inv_sum[h][:], p_dealt[h][:],
+            by_slot = "q (s r) -> q s r"
+            nc.vector.scalar_tensor_tensor(wb[:].rearrange("q r s -> q s r"), b[h][:].rearrange(by_slot, r=PACK), inv_sum[h][:], p_dealt[h][:].rearrange(by_slot, r=PACK),
                                            ALU.mult, ALU.mult, accum_out=mean[:])
             factor = tile("factor%d" % h, [P, 1], F32)
             neg_inv = tile("neg_inv%d" % h, [P, 1], F32)
@@ -140,7 +139,7 @@ def tile_attend_readtangent_pl_kernel(tc, query, dquery, keys_words, keys_scales
             nc.scalar.activation(factor[:], mean[:], ACT.Copy, scale=neg_inv[:])
             means.append(mean)
             wm = tile("wm%d" % h, [P, PACK, P], F32)
-            nc.scalar.activation(wm[:], p_dealt[h][:], ACT.Copy, scale=factor[:])
+            nc.scalar.activation(wm[:].rearrange("q r s -> q s r"), p_dealt[h][:].rearrange(by_slot, r=PACK), ACT.Copy, scale=factor[:])
             turned = ps.tile([P, PACK, P], F32, name="dw%d" % h, tag="a%d" % h)
             for r in range(PACK):
                 nc.tensor.matmul(turned[:, r, :], wb[:, r, :], ident[:], start=(r == 0), stop=False, is_transpose=True)

@@ -7,6 +7,13 @@ D, E, T, I, Q = 512, 512, 2048, 512, 256
 P = 128
 PACK = 4
 HALVES = Q // P
+QUADRANTS = 4
+LAST = PACK - 1
+CAST_PIECE = 512
+CAST_ON_SCALAR = 2
+REGION_BYTES = T * 4
+PART_BYTES = I * 4
+P_REGION = PACK
 FLOPS = 2 * (2 * D * Q * I + I * E * Q)
 
 F32 = mybir.dt.float32
@@ -27,16 +34,16 @@ def tile_attend_readtangent_pl_kernel(tc, query, dquery, keys_words, keys_scales
     with ExitStack() as ctx:
         sb = ctx.enter_context(tc.tile_pool(name="sb", bufs=1))
         ps = ctx.enter_context(tc.psum_pool(name="ps", bufs=1))
+        reused = ctx.enter_context(tc.tile_pool(name="reused", bufs=1))
 
-        shared = ctx.enter_context(tc.tile_pool(name="shared", bufs=1))
-
-        def tile(name, shape, dtype, place=None):
-            if place is None:
+        def tile(name, shape, dtype, spot=None):
+            if spot is None:
                 return sb.tile(shape, dtype, name=name, align_bytes=64)
-            return shared.tile(shape, dtype, name=name, align_bytes=64, offset=place[0] * T * 4 + place[1] * 2048)
+            region, part = spot
+            return reused.tile(shape, dtype, name=name, align_bytes=64, offset=region * REGION_BYTES + part * PART_BYTES)
 
-        def quantise(name, grouped, columns, tag=None):
-            codes = tile(name + "_codes", [P, columns], U32, tag)
+        def quantise(name, grouped, columns, spot=None):
+            codes = tile(name + "_codes", [P, columns], U32, spot)
             scales = tile(name + "_scales", [P, columns], U8)
             nc.vector.quantize_mx(out=codes[:].bitcast(FP8X4), scales=scales[:], in_=grouped)
             return codes, scales
@@ -45,170 +52,167 @@ def tile_attend_readtangent_pl_kernel(tc, query, dquery, keys_words, keys_scales
         key_bytes = tile("key_bytes", [P, T], U8)
         nc.gpsimd.memset(key_bytes[:].bitcast(I32), 0)
         nc.sync.dma_start(offsets[:], offs)
-        slot_size = tile("slot_size", [P, PACK], F32)
-        nc.sync.dma_start(slot_size[:], size.rearrange("o (s r) -> s (o r)", r=PACK))
-        for quad in range(4):
-            nc.sync.dma_start(key_bytes[32 * quad : 32 * quad + 4, :].bitcast(I32), keys_scales[0, 4 * quad : 4 * quad + 4, :].bitcast(I32))
         key_words = tile("key_words", [P, T], U16)
         nc.sync.dma_start(key_words[:].bitcast(I32), keys_words[0].bitcast(I32))
+        for quad in range(QUADRANTS):
+            nc.sync.dma_start(key_bytes[32 * quad : 32 * quad + 4, :].bitcast(I32), keys_scales[0, 4 * quad : 4 * quad + 4, :].bitcast(I32))
         q_raw = tile("q_raw", [P, PACK, Q], F32)
-        nc.sync.dma_start(q_raw[:], query.rearrange("(p j) q -> p j q", j=PACK))
+        nc.sync.dma_start(q_raw[:], query.rearrange("(p r) q -> p r q", r=PACK))
         dq_raw = tile("dq_raw", [P, PACK, Q], F32)
-        nc.sync.dma_start(dq_raw[:], dquery.rearrange("(p j) q -> p j q", j=PACK))
+        nc.sync.dma_start(dq_raw[:], dquery.rearrange("(p r) q -> p r q", r=PACK))
+        slot_size = tile("slot_size", [P, PACK], F32)
+        nc.sync.dma_start(slot_size[:], size.rearrange("o (s r) -> s (o r)", r=PACK))
         vals_rows = vals.rearrange("(p t) c -> t p c", t=PACK)
-        pools = []
+        value_tiles = []
         for t in range(PACK):
-            pool_t = tile("vals_pool%d" % t, [P, T], F32, (t, 0))
-            nc.sync.dma_start(pool_t[:], vals_rows[t])
-            pools.append(pool_t)
+            value_tile = tile("vals%d" % t, [P, T], F32, (t, 0))
+            nc.sync.dma_start(value_tile[:], vals_rows[t])
+            value_tiles.append(value_tile)
 
         ident = tile("ident", [P, P], F32)
         make_identity(nc, ident[:])
 
-        kb = tile("kb", [P, I], U8)
-        nc.vector.tensor_copy(kb[:], key_bytes[:].indirect(offsets[:]))
+        listed_words = tile("listed_words", [P, I], U16)
+        nc.vector.tensor_copy(listed_words[:], key_words[:].indirect(offsets[:]))
+        listed_bytes = tile("listed_bytes", [P, I], U8)
+        nc.vector.tensor_copy(listed_bytes[:], key_bytes[:].indirect(offsets[:]))
 
-        def interleave(name, rows, on_vector=False):
+        def round_queries(name, rows):
             grouped = tile(name, [P, P, PACK], BF16)
-            dst = grouped[:].rearrange("p (c i) j -> p c j i", i=4)
-            src = rows.rearrange("p j (c i) -> p c j i", i=4)
-            if on_vector:
-                nc.vector.tensor_copy(dst, src)
-            else:
-                nc.scalar.activation(dst, src, ACT.Copy)
-            return grouped[:].rearrange("p q j -> p (q j)")
+            nc.scalar.activation(grouped[:].rearrange("p (c n) r -> p c r n", n=4), rows.rearrange("p r (c n) -> p c r n", n=4), ACT.Copy)
+            return grouped[:].rearrange("p q r -> p (q r)")
 
-        kw = tile("kw", [P, I], U16)
-        nc.vector.tensor_copy(kw[:], key_words[:].indirect(offsets[:]))
-        q_bf = [interleave("q_bf%d" % h, q_raw[:, :, h * P : (h + 1) * P], h == 0) for h in range(HALVES)]
-        dq_bf = [interleave("dq_bf%d" % h, dq_raw[:, :, h * P : (h + 1) * P]) for h in range(HALVES)]
+        q_bf = [round_queries("q_bf%d" % h, q_raw[:, :, h * P : (h + 1) * P]) for h in range(HALVES)]
+        dq_bf = [round_queries("dq_bf%d" % h, dq_raw[:, :, h * P : (h + 1) * P]) for h in range(HALVES)]
 
-        def scores(tag, grouped):
-            codes, scales = quantise(tag, grouped, P)
-            bank = ps.tile([P, I], F32, name=tag, tag=tag)
+        def scores(bank_tag, grouped):
+            codes, scales = quantise(bank_tag, grouped, P)
+            bank = ps.tile([P, I], F32, name=bank_tag, tag=bank_tag)
             nc.tensor.matmul_mx(out=bank[:], lhsT=codes[:].bitcast(FP8X4), lhsT_scale=scales[:],
-                                rhs=kw[:].bitcast(FP4X4), rhs_scale=kb[:], start=True, stop=True)
+                                rhs=listed_words[:].bitcast(FP4X4), rhs_scale=listed_bytes[:], start=True, stop=True)
             return bank
 
         a = [scores("a%d" % h, q_bf[h]) for h in range(HALVES)]
-        p_dealt, inv_sum, b = [], [], []
-
-        def softmax(h):
+        p, inv_sum, b = [], [], []
+        for h in range(HALVES):
             neg_max = tile("neg_max%d" % h, [P, 1], F32)
             nc.vector.tensor_reduce(neg_max[:], a[h][:], AXIS.X, ALU.max, negate=True)
-            p_h = tile("p%d" % h, [P, I], F32, (PACK, h))
+            p_h = tile("p%d" % h, [P, I], F32, (P_REGION, h))
             row_sum = tile("row_sum%d" % h, [P, 1], F32)
             nc.scalar.activation(p_h[:], a[h][:], ACT.Exp, bias=neg_max[:], accum_out=row_sum[:])
             inv = tile("inv_sum%d" % h, [P, 1], F32)
             nc.vector.reciprocal(inv[:], row_sum[:])
-            p_dealt.append(p_h)
+            p.append(p_h)
             inv_sum.append(inv)
+            b.append(scores("b%d" % h, dq_bf[h]))
 
-        softmax(0)
-        b.append(scores("b0", dq_bf[0]))
-        softmax(1)
-        b.append(scores("b1", dq_bf[1]))
-
-        picks = []
+        listed_values = {}
 
         def gather_values(t):
-            picked = tile("picked%d" % t, [P, I], BF16)
-            nc.vector.tensor_copy(picked[:], pools[t][:].indirect(offsets[:]))
-            picks.append(picked)
+            listed_values[t] = tile("listed_values%d" % t, [P, I], BF16)
+            nc.vector.tensor_copy(listed_values[t][:], value_tiles[t][:].indirect(offsets[:]))
 
-        def turn_values(t, bank):
-            turned = ps.tile([P, 2, P], F32, name="turned%d" % t, tag=bank)
-            words = picks[t][:].bitcast(F32)
+        def turn_values(t, bank_tag):
+            turned = ps.tile([P, 2, P], F32, name="turned%d" % t, tag=bank_tag)
+            words = listed_values[t][:].bitcast(F32)
             for u in range(2):
                 nc.tensor.transpose(turned[:, u, :], words[:, u::2], ident[:])
             grouped = tile("v_bf%d" % t, [P, P, 2], F32)
             nc.scalar.copy(grouped[:], turned[:].rearrange("s u e -> s e u"))
             return grouped[:].rearrange("s e u -> s (e u)").bitcast(BF16)
 
-        means = []
+        by_slot = "q (s r) -> q s r"
+        by_place = "q r s -> q s r"
 
-        def tangent(h):
+        def first_term(h):
             wb = tile("wb%d" % h, [P, PACK, P], F32)
             mean = tile("mean%d" % h, [P, 1], F32)
-            by_slot = "q (s r) -> q s r"
-            nc.vector.scalar_tensor_tensor(wb[:].rearrange("q r s -> q s r"), b[h][:].rearrange(by_slot, r=PACK), inv_sum[h][:], p_dealt[h][:].rearrange(by_slot, r=PACK),
-                                           ALU.mult, ALU.mult, accum_out=mean[:])
-            factor = tile("factor%d" % h, [P, 1], F32)
+            nc.vector.scalar_tensor_tensor(wb[:].rearrange(by_place), b[h][:].rearrange(by_slot, r=PACK), inv_sum[h][:],
+                                           p[h][:].rearrange(by_slot, r=PACK), ALU.mult, ALU.mult, accum_out=mean[:])
             neg_inv = tile("neg_inv%d" % h, [P, 1], F32)
             nc.scalar.activation(neg_inv[:], inv_sum[h][:], ACT.Copy, scale=-1.0)
-            nc.scalar.activation(factor[:], mean[:], ACT.Copy, scale=neg_inv[:])
-            means.append(mean)
-            wm = tile("wm%d" % h, [P, PACK, P], F32)
-            nc.scalar.activation(wm[:].rearrange("q r s -> q s r"), p_dealt[h][:].rearrange(by_slot, r=PACK), ACT.Copy, scale=factor[:])
             turned = ps.tile([P, PACK, P], F32, name="dw%d" % h, tag="a%d" % h)
             for r in range(PACK):
                 nc.tensor.matmul(turned[:, r, :], wb[:, r, :], ident[:], start=(r == 0), stop=False, is_transpose=True)
+            return turned, mean, neg_inv
+
+        def second_term(h, turned, mean, neg_inv, spot=None):
+            factor = tile("factor%d" % h, [P, 1], F32)
+            nc.scalar.activation(factor[:], mean[:], ACT.Copy, scale=neg_inv[:])
+            wm = tile("wm%d" % h, [P, PACK, P], F32, spot)
+            nc.scalar.activation(wm[:].rearrange(by_place), p[h][:].rearrange(by_slot, r=PACK), ACT.Copy, scale=factor[:])
             for r in range(PACK):
                 nc.tensor.matmul(turned[:, r, :], wm[:, r, :], ident[:], start=False, stop=(r == PACK - 1), is_transpose=True)
             return turned
 
-        w_bf = tile("w_bf", [P, Q, PACK], BF16)
-
-        def weigh(h, turned):
-            nc.vector.tensor_tensor(w_bf[:, h * P : (h + 1) * P, :], turned[:].rearrange("s r q -> s q r"),
+        def weigh(h, turned, spot=None):
+            grouped = tile("w_bf%d" % h, [P, P, PACK], BF16, spot)
+            nc.vector.tensor_tensor(grouped[:], turned[:].rearrange("s r q -> s q r"),
                                     slot_size[:].unsqueeze(1).to_broadcast([P, P, PACK]), ALU.mult)
+            return grouped[:].rearrange("s q r -> s (q r)")
 
-        dw = [tangent(h) for h in range(HALVES)]
-        pool0_bf = tile("pool0_bf", [P, T], BF16)
-        nc.vector.tensor_copy(pool0_bf[:, T // 2 :], pools[0][:, T // 2 :])
-        for c in range(2):
-            nc.scalar.copy(pool0_bf[:, 512 * c : 512 * (c + 1)], pools[0][:, 512 * c : 512 * (c + 1)])
-        picked0 = tile("picked0", [P, I], BF16, (PACK, 1))
-        picks.append(picked0)
+        dw0 = second_term(0, *first_term(0))
+        begun1 = first_term(1)
+
+        vals0_bf = tile("vals0_bf", [P, T], BF16)
+        split = CAST_ON_SCALAR * CAST_PIECE
+        nc.vector.tensor_copy(vals0_bf[:, split:], value_tiles[0][:, split:])
+        for piece in range(CAST_ON_SCALAR):
+            cols = slice(piece * CAST_PIECE, (piece + 1) * CAST_PIECE)
+            nc.scalar.copy(vals0_bf[:, cols], value_tiles[0][:, cols])
+        listed_values[0] = tile("listed_values0", [P, I], BF16, (P_REGION, 0))
         gather_values(1)
-        for h in range(HALVES):
-            weigh(h, dw[h])
+        w_bf0 = weigh(0, dw0)
+        nc.scalar.activation(listed_values[0][:], vals0_bf[:].indirect(offsets[:]), ACT.Copy)
         v_bf = {1: turn_values(1, "b0")}
-        nc.scalar.activation(picked0[:], pool0_bf[:].indirect(offsets[:]), ACT.Copy)
-        v_mx = {1: quantise("v1", v_bf[1], P)}
-        w_codes, w_scales = quantise("w", w_bf[:].rearrange("s q r -> s (q r)"), Q)
         v_bf[0] = turn_values(0, "v0")
+        dw1 = second_term(1, *begun1, spot=(P_REGION, 0))
+
         gather_values(2)
-        v_mx[0] = quantise("v0", v_bf[0], P)
+        w_mx = [quantise("w0", w_bf0, P)]
+        v_mx = {1: quantise("v1", v_bf[1], P, (2, 0))}
+        v_mx[0] = quantise("v0", v_bf[0], P, (2, 1))
         v_bf[2] = turn_values(2, "b1")
 
         o_bank = [ps.tile([P, PACK, P], F32, name="o%d" % h, tag="o%d" % h) for h in range(HALVES)]
 
-        def read_out(t):
+        def read_out(t, h):
             v_codes, v_scales = v_mx[t]
-            for h in range(HALVES):
-                cols = slice(h * P, (h + 1) * P)
-                nc.tensor.matmul_mx(out=o_bank[h][:, t, :], lhsT=v_codes[:].bitcast(FP8X4), lhsT_scale=v_scales[:],
-                                    rhs=w_codes[:, cols].bitcast(FP8X4), rhs_scale=w_scales[:, cols], start=True, stop=True)
+            w_codes, w_scales = w_mx[h]
+            nc.tensor.matmul_mx(out=o_bank[h][:, t, :], lhsT=v_codes[:].bitcast(FP8X4), lhsT_scale=v_scales[:],
+                                rhs=w_codes[:].bitcast(FP8X4), rhs_scale=w_scales[:], start=True, stop=True)
 
         out_rows = out_0.rearrange("(p t) q -> p t q", t=PACK)
-        last = PACK - 1
+        low, high = slice(0, 2), slice(2, PACK)
+        read_out(1, 0)
+        read_out(0, 0)
+        o_low = [tile("o_low%d" % h, [P, 2, P], F32) for h in range(HALVES)]
+        nc.scalar.copy(o_low[0][:], o_bank[0][:, low, :])
+        nc.sync.dma_start(out_rows[:, low, 0:P], o_low[0][:])
 
-        def hand_out(name, first, stop):
-            rows = tile(name, [P, stop - first, Q], F32)
-            for h in range(HALVES):
-                nc.scalar.copy(rows[:, :, h * P : (h + 1) * P], o_bank[h][:, first:stop, :])
-            nc.sync.dma_start(out_rows[:, first:stop, :], rows[:])
+        gather_values(LAST)
+        v_bf[LAST] = turn_values(LAST, "v3")
+        w_bf1 = weigh(1, dw1, (LAST, 0))
+        v_mx[2] = quantise("v2", v_bf[2], P, (LAST, 1))
+        w_mx.append(quantise("w1", w_bf1, P))
+        v_mx[LAST] = quantise("v3", v_bf[LAST], P)
+        read_out(2, 0)
+        for t in range(LAST):
+            read_out(t, 1)
+        for h in range(HALVES):
+            read_out(LAST, h)
 
-        read_out(1)
-        read_out(0)
-        hand_out("o_01", 0, 2)
-        gather_values(last)
-        v_bf[last] = turn_values(last, "v3")
-        v_mx[2] = quantise("v2", v_bf[2], P, (last, 0))
-        read_out(2)
-        hand_out("o_2", 2, 3)
-        v_mx[last] = quantise("v3", v_bf[last], P)
-        read_out(last)
         o_bf = tile("o_bf", [P, Q, PACK], BF16)
+        o_high = tile("o_high", [P, 2, Q], F32)
         nc.vector.tensor_copy(o_bf[:, 0:P, :], o_bank[0][:].rearrange("p t q -> p q t"))
         nc.scalar.copy(o_bf[:, P:Q, :], o_bank[1][:].rearrange("p t q -> p q t"))
+        nc.vector.tensor_copy(o_high[:, :, 0:P], o_bank[0][:, high, :])
         o_codes, o_scales = quantise("o", o_bf[:].rearrange("p q t -> p (q t)"), Q)
-        o_last = tile("o_last", [P, Q], F32)
-        for h in reversed(range(HALVES)):
-            nc.scalar.copy(o_last[:, h * P : (h + 1) * P], o_bank[h][:, last, :])
-        nc.scalar.dma_start(out_rows[:, last, :], o_last[:])
+        nc.scalar.copy(o_high[:, :, P:Q], o_bank[1][:, high, :])
+        nc.scalar.dma_start(out_rows[:, high, :], o_high[:])
+        nc.scalar.copy(o_low[1][:], o_bank[1][:, low, :])
+        nc.scalar.dma_start(out_rows[:, low, P:Q], o_low[1][:])
         nc.sync.dma_start(out_1[0].rearrange("p c r -> p (c r)").bitcast(I32), o_codes[:].bitcast(I32))
-        for quad in range(4):
+        for quad in range(QUADRANTS):
             queue = nc.sync if quad % 2 == 0 else nc.scalar
             queue.dma_start(out_2[0, 4 * quad : 4 * quad + 4, :].bitcast(I32), o_scales[32 * quad : 32 * quad + 4, :].bitcast(I32))

from contextlib import ExitStack

import concourse.mybir as mybir
from concourse.masks import make_identity

D, E, T, I, Q = 512, 512, 2048, 512, 256
P = 128
PACK = 4
HALVES = Q // P
QUADRANTS = 4
LAST = PACK - 1
CAST_PIECE = 512
CAST_ON_SCALAR = 2
REGION_BYTES = T * 4
PART_BYTES = I * 4
P_REGION = PACK
FLOPS = 2 * (2 * D * Q * I + I * E * Q)

F32 = mybir.dt.float32
BF16 = mybir.dt.bfloat16
I32 = mybir.dt.int32
U32 = mybir.dt.uint32
U16 = mybir.dt.uint16
U8 = mybir.dt.uint8
FP8X4 = mybir.dt.float8_e4m3fn_x4
FP4X4 = mybir.dt.float4_e2m1fn_x4
ALU = mybir.AluOpType
ACT = mybir.ActivationFunctionType
AXIS = mybir.AxisListType


def tile_attend_readtangent_pl_kernel(tc, query, dquery, keys_words, keys_scales, size, vals, offs, out_0, out_1, out_2):
    nc = tc.nc
    with ExitStack() as ctx:
        sb = ctx.enter_context(tc.tile_pool(name="sb", bufs=1))
        ps = ctx.enter_context(tc.psum_pool(name="ps", bufs=1))
        reused = ctx.enter_context(tc.tile_pool(name="reused", bufs=1))

        def tile(name, shape, dtype, spot=None):
            if spot is None:
                return sb.tile(shape, dtype, name=name, align_bytes=64)
            region, part = spot
            return reused.tile(shape, dtype, name=name, align_bytes=64, offset=region * REGION_BYTES + part * PART_BYTES)

        def quantise(name, grouped, columns, spot=None):
            codes = tile(name + "_codes", [P, columns], U32, spot)
            scales = tile(name + "_scales", [P, columns], U8)
            nc.vector.quantize_mx(out=codes[:].bitcast(FP8X4), scales=scales[:], in_=grouped)
            return codes, scales

        offsets = sb.tile([P, I // 16], U16, name="offsets")
        key_bytes = tile("key_bytes", [P, T], U8)
        nc.gpsimd.memset(key_bytes[:].bitcast(I32), 0)
        nc.sync.dma_start(offsets[:], offs)
        key_words = tile("key_words", [P, T], U16)
        nc.sync.dma_start(key_words[:].bitcast(I32), keys_words[0].bitcast(I32))
        for quad in range(QUADRANTS):
            nc.sync.dma_start(key_bytes[32 * quad : 32 * quad + 4, :].bitcast(I32), keys_scales[0, 4 * quad : 4 * quad + 4, :].bitcast(I32))
        q_raw = tile("q_raw", [P, PACK, Q], F32)
        nc.sync.dma_start(q_raw[:], query.rearrange("(p r) q -> p r q", r=PACK))
        dq_raw = tile("dq_raw", [P, PACK, Q], F32)
        nc.sync.dma_start(dq_raw[:], dquery.rearrange("(p r) q -> p r q", r=PACK))
        slot_size = tile("slot_size", [P, PACK], F32)
        nc.sync.dma_start(slot_size[:], size.rearrange("o (s r) -> s (o r)", r=PACK))
        vals_rows = vals.rearrange("(p t) c -> t p c", t=PACK)
        value_tiles = []
        for t in range(PACK):
            value_tile = tile("vals%d" % t, [P, T], F32, (t, 0))
            nc.sync.dma_start(value_tile[:], vals_rows[t])
            value_tiles.append(value_tile)

        ident = tile("ident", [P, P], F32)
        make_identity(nc, ident[:])

        listed_words = tile("listed_words", [P, I], U16)
        nc.vector.tensor_copy(listed_words[:], key_words[:].indirect(offsets[:]))
        listed_bytes = tile("listed_bytes", [P, I], U8)
        nc.vector.tensor_copy(listed_bytes[:], key_bytes[:].indirect(offsets[:]))

        def round_queries(name, rows):
            grouped = tile(name, [P, P, PACK], BF16)
            nc.scalar.activation(grouped[:].rearrange("p (c n) r -> p c r n", n=4), rows.rearrange("p r (c n) -> p c r n", n=4), ACT.Copy)
            return grouped[:].rearrange("p q r -> p (q r)")

        q_bf = [round_queries("q_bf%d" % h, q_raw[:, :, h * P : (h + 1) * P]) for h in range(HALVES)]
        dq_bf = [round_queries("dq_bf%d" % h, dq_raw[:, :, h * P : (h + 1) * P]) for h in range(HALVES)]

        def scores(bank_tag, grouped):
            codes, scales = quantise(bank_tag, grouped, P)
            bank = ps.tile([P, I], F32, name=bank_tag, tag=bank_tag)
            nc.tensor.matmul_mx(out=bank[:], lhsT=codes[:].bitcast(FP8X4), lhsT_scale=scales[:],
                                rhs=listed_words[:].bitcast(FP4X4), rhs_scale=listed_bytes[:], start=True, stop=True)
            return bank

        a = [scores("a%d" % h, q_bf[h]) for h in range(HALVES)]
        p, inv_sum, b = [], [], []
        for h in range(HALVES):
            neg_max = tile("neg_max%d" % h, [P, 1], F32)
            nc.vector.tensor_reduce(neg_max[:], a[h][:], AXIS.X, ALU.max, negate=True)
            p_h = tile("p%d" % h, [P, I], F32, (P_REGION, h))
            row_sum = tile("row_sum%d" % h, [P, 1], F32)
            nc.scalar.activation(p_h[:], a[h][:], ACT.Exp, bias=neg_max[:], accum_out=row_sum[:])
            inv = tile("inv_sum%d" % h, [P, 1], F32)
            nc.vector.reciprocal(inv[:], row_sum[:])
            p.append(p_h)
            inv_sum.append(inv)
            b.append(scores("b%d" % h, dq_bf[h]))

        listed_values = {}

        def gather_values(t):
            listed_values[t] = tile("listed_values%d" % t, [P, I], BF16)
            nc.vector.tensor_copy(listed_values[t][:], value_tiles[t][:].indirect(offsets[:]))

        def turn_values(t, bank_tag):
            turned = ps.tile([P, 2, P], F32, name="turned%d" % t, tag=bank_tag)
            words = listed_values[t][:].bitcast(F32)
            for u in range(2):
                nc.tensor.transpose(turned[:, u, :], words[:, u::2], ident[:])
            grouped = tile("v_bf%d" % t, [P, P, 2], F32)
            nc.scalar.copy(grouped[:], turned[:].rearrange("s u e -> s e u"))
            return grouped[:].rearrange("s e u -> s (e u)").bitcast(BF16)

        by_slot = "q (s r) -> q s r"
        by_place = "q r s -> q s r"

        def first_term(h):
            wb = tile("wb%d" % h, [P, PACK, P], F32)
            mean = tile("mean%d" % h, [P, 1], F32)
            nc.vector.scalar_tensor_tensor(wb[:].rearrange(by_place), b[h][:].rearrange(by_slot, r=PACK), inv_sum[h][:],
                                           p[h][:].rearrange(by_slot, r=PACK), ALU.mult, ALU.mult, accum_out=mean[:])
            neg_inv = tile("neg_inv%d" % h, [P, 1], F32)
            nc.scalar.activation(neg_inv[:], inv_sum[h][:], ACT.Copy, scale=-1.0)
            turned = ps.tile([P, PACK, P], F32, name="dw%d" % h, tag="a%d" % h)
            for r in range(PACK):
                nc.tensor.matmul(turned[:, r, :], wb[:, r, :], ident[:], start=(r == 0), stop=False, is_transpose=True)
            return turned, mean, neg_inv

        def second_term(h, turned, mean, neg_inv, spot=None):
            factor = tile("factor%d" % h, [P, 1], F32)
            nc.scalar.activation(factor[:], mean[:], ACT.Copy, scale=neg_inv[:])
            wm = tile("wm%d" % h, [P, PACK, P], F32, spot)
            nc.scalar.activation(wm[:].rearrange(by_place), p[h][:].rearrange(by_slot, r=PACK), ACT.Copy, scale=factor[:])
            for r in range(PACK):
                nc.tensor.matmul(turned[:, r, :], wm[:, r, :], ident[:], start=False, stop=(r == PACK - 1), is_transpose=True)
            return turned

        def weigh(h, turned, spot=None):
            grouped = tile("w_bf%d" % h, [P, P, PACK], BF16, spot)
            nc.vector.tensor_tensor(grouped[:], turned[:].rearrange("s r q -> s q r"),
                                    slot_size[:].unsqueeze(1).to_broadcast([P, P, PACK]), ALU.mult)
            return grouped[:].rearrange("s q r -> s (q r)")

        dw0 = second_term(0, *first_term(0))
        begun1 = first_term(1)

        vals0_bf = tile("vals0_bf", [P, T], BF16)
        split = CAST_ON_SCALAR * CAST_PIECE
        nc.vector.tensor_copy(vals0_bf[:, split:], value_tiles[0][:, split:])
        for piece in range(CAST_ON_SCALAR):
            cols = slice(piece * CAST_PIECE, (piece + 1) * CAST_PIECE)
            nc.scalar.copy(vals0_bf[:, cols], value_tiles[0][:, cols])
        listed_values[0] = tile("listed_values0", [P, I], BF16, (P_REGION, 0))
        gather_values(1)
        w_bf0 = weigh(0, dw0)
        nc.scalar.activation(listed_values[0][:], vals0_bf[:].indirect(offsets[:]), ACT.Copy)
        v_bf = {1: turn_values(1, "b0")}
        v_bf[0] = turn_values(0, "v0")
        dw1 = second_term(1, *begun1, spot=(P_REGION, 0))

        gather_values(2)
        w_mx = [quantise("w0", w_bf0, P)]
        v_mx = {1: quantise("v1", v_bf[1], P, (2, 0))}
        v_mx[0] = quantise("v0", v_bf[0], P, (2, 1))
        v_bf[2] = turn_values(2, "b1")

        o_bank = [ps.tile([P, PACK, P], F32, name="o%d" % h, tag="o%d" % h) for h in range(HALVES)]

        def read_out(t, h):
            v_codes, v_scales = v_mx[t]
            w_codes, w_scales = w_mx[h]
            nc.tensor.matmul_mx(out=o_bank[h][:, t, :], lhsT=v_codes[:].bitcast(FP8X4), lhsT_scale=v_scales[:],
                                rhs=w_codes[:].bitcast(FP8X4), rhs_scale=w_scales[:], start=True, stop=True)

        out_rows = out_0.rearrange("(p t) q -> p t q", t=PACK)
        low, high = slice(0, 2), slice(2, PACK)
        read_out(1, 0)
        read_out(0, 0)
        o_low = [tile("o_low%d" % h, [P, 2, P], F32) for h in range(HALVES)]
        nc.scalar.copy(o_low[0][:], o_bank[0][:, low, :])
        nc.sync.dma_start(out_rows[:, low, 0:P], o_low[0][:])

        gather_values(LAST)
        v_bf[LAST] = turn_values(LAST, "v3")
        w_bf1 = weigh(1, dw1, (LAST, 0))
        v_mx[2] = quantise("v2", v_bf[2], P, (LAST, 1))
        w_mx.append(quantise("w1", w_bf1, P))
        v_mx[LAST] = quantise("v3", v_bf[LAST], P)
        read_out(2, 0)
        for t in range(LAST):
            read_out(t, 1)
        for h in range(HALVES):
            read_out(LAST, h)

        o_bf = tile("o_bf", [P, Q, PACK], BF16)
        o_high = tile("o_high", [P, 2, Q], F32)
        nc.vector.tensor_copy(o_bf[:, 0:P, :], o_bank[0][:].rearrange("p t q -> p q t"))
        nc.scalar.copy(o_bf[:, P:Q, :], o_bank[1][:].rearrange("p t q -> p q t"))
        nc.vector.tensor_copy(o_high[:, :, 0:P], o_bank[0][:, high, :])
        o_codes, o_scales = quantise("o", o_bf[:].rearrange("p q t -> p (q t)"), Q)
        nc.scalar.copy(o_high[:, :, P:Q], o_bank[1][:, high, :])
        nc.scalar.dma_start(out_rows[:, high, :], o_high[:])
        nc.scalar.copy(o_low[1][:], o_bank[1][:, low, :])
        nc.scalar.dma_start(out_rows[:, low, P:Q], o_low[1][:])
        nc.sync.dma_start(out_1[0].rearrange("p c r -> p (c r)").bitcast(I32), o_codes[:].bitcast(I32))
        for quad in range(QUADRANTS):
            queue = nc.sync if quad % 2 == 0 else nc.scalar
            queue.dma_start(out_2[0, 4 * quad : 4 * quad + 4, :].bitcast(I32), o_scales[32 * quad : 32 * quad + 4, :].bitcast(I32))
